import numpy as np
import ml_dtypes


def mxq(x, axis, fmt="e4m3"):
    dtype, down = {"e4m3": (ml_dtypes.float8_e4m3fn, 7), "e5m2": (ml_dtypes.float8_e5m2, 14)}[fmt]
    v = np.moveaxis(np.asarray(x, np.float32).astype(ml_dtypes.bfloat16).astype(np.float64), axis, -1)
    blocks = v.reshape(v.shape[:-1] + (-1, 32))
    amax = np.abs(blocks).max(-1, keepdims=True)
    byte = np.maximum(np.where(amax > 0, np.frexp(amax)[1] - 1 + 127, 0) - down, 1)
    scale = np.exp2(byte - 127.0)
    codes = (blocks / scale).astype(np.float32).astype(dtype).astype(np.float64)
    return np.moveaxis((codes * scale).reshape(v.shape), -1, axis)


WIDE = False


def mx_kscale(k):
    if not WIDE:
        return np.ones(k)
    levels = np.array([30, -30])
    if k % 512:
        return np.exp2(np.random.permutation(np.resize(levels, k // 32))).repeat(32)
    a = np.empty((k // 512, 16))
    for p in range(k // 512):
        a[p, :8] = np.random.permutation(np.resize(levels, 8))
        for g in range(8):
            far = levels[np.abs(levels - a[p, g]) >= 10]
            a[p, g + 8] = far[np.random.randint(len(far))]
    return np.exp2(a.ravel()).repeat(32)


def f64(x):
    return np.asarray(x).astype(np.float64)


def striped(idx):
    return np.tile(np.asarray(idx).reshape(-1, 16).T, (8, 1)).astype(np.uint16)


def unstriped(offs):
    return offs[:16].T.reshape(-1).astype(np.int64)


def striped8(idx):
    return np.asarray(idx).reshape(8, -1, 16).transpose(0, 2, 1).reshape(128, -1).astype(np.uint16)


def unstriped8(offs):
    return offs.reshape(8, 16, -1).transpose(0, 2, 1).reshape(8, -1).astype(np.int64)


def pick8(x, idx, run):
    r = np.arange(len(x))
    return x[r[:, None], idx[r % (8 * run) // run]]


E2M1 = np.array([0.0, 0.5, 1.0, 1.5, 2.0, 3.0, 4.0, 6.0, -0.0, -0.5, -1.0, -1.5, -2.0, -3.0, -4.0, -6.0])


def pack_weight(w, fmt):
    k, n = w.shape
    w = f64(np.asarray(w, np.float32).astype(ml_dtypes.bfloat16)).reshape(k // 32, 32, n)
    amax = np.abs(w).max(1)
    if fmt in ("e4m3", "e5m2"):
        byte = np.frexp(amax)[1] - 1 + 127 - (7 if fmt == "e4m3" else 14)
    else:
        mant, ex = np.frexp(amax / 6.0)
        byte = np.where(mant > 0.5, ex, ex - 1) + 127
    byte = np.clip(np.where(amax > 0, byte, 1), 1, 254)
    scaled = (w * np.exp2(127.0 - byte)[:, None, :]).reshape(k, n).astype(np.float32)
    by_word = np.ascontiguousarray(scaled.reshape(k // 512, 128, 4, n).transpose(0, 1, 3, 2))
    if fmt in ("e4m3", "e5m2"):
        words = by_word.astype(ml_dtypes.float8_e4m3fn if fmt == "e4m3" else ml_dtypes.float8_e5m2).view(np.uint8)
    else:
        c = by_word.astype(ml_dtypes.float4_e2m1fn).view(np.uint8) & 0xF
        words = (c[..., 0::2] | (c[..., 1::2] << 4)).reshape(k // 512, 128, 2 * n)
    return np.ascontiguousarray(words), np.ascontiguousarray(byte.astype(np.uint8).reshape(k // 512, 16, n))


def unpack_weight(words, scales, fmt):
    g, _, n = scales.shape
    words = np.ascontiguousarray(words).reshape(g, 128, n, -1)
    if fmt in ("e4m3", "e5m2"):
        vals = words.view(ml_dtypes.float8_e4m3fn if fmt == "e4m3" else ml_dtypes.float8_e5m2).astype(np.float64)
    else:
        nib = np.empty((g, 128, n, 4), np.uint8)
        nib[..., 0::2] = words & 0xF
        nib[..., 1::2] = words >> 4
        vals = E2M1[nib]
    vals = vals * np.repeat(np.exp2(scales.astype(np.float64) - 127.0), 8, axis=1)[..., None]
    return vals.transpose(0, 1, 3, 2).reshape(g * 512, n)


K, T, J, R, F, Z, C, O, N, S, E = 512, 1024, 256, 512, 512, 1024, 512, 128, 256, 1024, 1024


def setup_inputs():
    n = np.random.standard_normal
    idx = np.random.permutation(T)[:J]
    idx2 = np.random.permutation(Z)[:J]
    idx3 = np.stack([np.random.permutation(C)[:J] for _ in range(8)])
    idx4 = np.stack([np.random.permutation(C)[:O] for _ in range(8)])
    idx5 = np.random.permutation(J)[:O]
    idx6 = np.random.permutation(S)[:N]
    idx7 = np.random.permutation(E)[:O]
    fk = mx_kscale(K)
    ff = mx_kscale(F)
    fr = mx_kscale(R)
    xtp = pack_weight(n((K, T)) / fk[:, None], "e2m1")
    xop = pack_weight(n((F, Z)) / ff[:, None], "e5m2")
    wp = pack_weight(n((K, R)) * 1 / np.sqrt(K) * fk[:, None] * fr, "e5m2")
    w0p = pack_weight(n((F, R)) * 1 / np.sqrt(F) * ff[:, None] * fr, "e4m3")
    w2p = pack_weight(n((F, R)) * 1 / np.sqrt(F) * ff[:, None], "e4m3")
    vsp = pack_weight(n((R, S)) * 1 / np.sqrt(R) / fr[:, None], "e4m3")
    return {
        "xt_words": xtp[0],
        "xt_scales": xtp[1],
        "xo_words": xop[0],
        "xo_scales": xop[1],
        "w_words": wp[0],
        "w_scales": wp[1],
        "w0_words": w0p[0],
        "w0_scales": w0p[1],
        "w2_words": w2p[0],
        "w2_scales": w2p[1],
        "vs_words": vsp[0],
        "vs_scales": vsp[1],
        "offs": striped(idx),
        "offs2": striped(idx2),
        "offs3": striped8(idx3),
        "offs4": striped8(idx4),
        "offs5": striped(idx5),
        "offs6": striped(idx6),
        "offs7": striped(idx7),
    }


def reference(xt_words, xt_scales, xo_words, xo_scales, w_words, w_scales, w0_words, w0_scales, w2_words, w2_scales, vs_words, vs_scales, offs, offs2, offs3, offs4, offs5, offs6, offs7):
    idx = unstriped(offs)
    idx2 = unstriped(offs2)
    idx3 = unstriped8(offs3)
    idx4 = unstriped8(offs4)
    idx5 = unstriped(offs5)
    idx6 = unstriped(offs6)
    idx7 = unstriped(offs7)
    xtu = unpack_weight(xt_words, xt_scales, "e2m1")
    xou = unpack_weight(xo_words, xo_scales, "e5m2")
    wu = unpack_weight(w_words, w_scales, "e5m2")
    w0u = unpack_weight(w0_words, w0_scales, "e4m3")
    w2u = unpack_weight(w2_words, w2_scales, "e4m3")
    vsu = unpack_weight(vs_words, vs_scales, "e4m3")
    xtidxg = xtu[:, idx]
    xoidx2g = xou[:, idx2]
    a = wu.T @ xtidxg + w0u.T @ xoidx2g
    b = w2u.T @ xoidx2g
    lb = b[:, 0:1]
    la = a[:, 0:1]
    pw = np.zeros((R, C))
    pw[np.arange(R)[:, None], idx3[np.arange(R) % 512 // 64]] = a
    hid = np.abs(pick8(pw, idx4, 64) * lb - b[:, idx5] * la)
    vsidx6g = vsu[:, idx6]
    hidq = mxq(hid, 0, "e5m2")
    p = vsidx6g.T @ hidq
    y = np.zeros((N, E))
    y[:, idx7] = p
    return y

@@ -1,0 +1,184 @@
+from contextlib import ExitStack
+
+import concourse.mybir as mybir
+
+K, T, J, R, F, Z, C, O, N, S, E = 512, 1024, 256, 512, 512, 1024, 512, 128, 256, 1024, 1024
+FLOPS = 2 * K * R * J + 2 * 2 * F * R * J + 2 * R * N * O
+
+F32 = mybir.dt.float32
+BF16 = mybir.dt.bfloat16
+I32 = mybir.dt.int32
+U32 = mybir.dt.uint32
+U16 = mybir.dt.uint16
+U8 = mybir.dt.uint8
+E4M3 = mybir.dt.float8_e4m3fn_x4
+E5M2 = mybir.dt.float8_e5m2_x4
+E2M1 = mybir.dt.float4_e2m1fn_x4
+ACT = mybir.ActivationFunctionType
+ALU = mybir.AluOpType
+
+P = 128
+PACK = 4
+QUADS = 4
+
+
+def tile_list_leadgroupboard_noted_store_scattered_kernel(
+    tc, xt_words, xt_scales, xo_words, xo_scales, w_words, w_scales, w0_words, w0_scales,
+    w2_words, w2_scales, vs_words, vs_scales, offs, offs2, offs3, offs4, offs5, offs6, offs7, out,
+):
+    nc = tc.nc
+    with ExitStack() as ctx:
+        keep = ctx.enter_context(tc.tile_pool(name="keep", bufs=1))
+        psum = ctx.enter_context(tc.psum_pool(name="psum", bufs=1))
+
+        def new(shape, dtype, name):
+            return keep.tile(shape, dtype, name=name, align_bytes=64)
+
+        def load_list(src, name):
+            lst = keep.tile(list(src.shape), U16, name=name)
+            nc.sync.dma_start(lst[:], src)
+            return lst
+
+        def load_words(src, columns, dtype, name):
+            words = new([P, columns], dtype, name)
+            rows = src[0] if src.ndim == 3 else src[0].rearrange("p n t -> p (n t)")
+            nc.sync.dma_start(words[:].bitcast(I32), rows.bitcast(I32))
+            return words
+
+        def load_plane(queue, plane, src):
+            for q in range(QUADS):
+                queue.dma_start(plane[32 * q : 32 * q + 4].bitcast(I32), src[0, 4 * q : 4 * q + 4, :].bitcast(I32))
+
+        xo_plane = new([P, Z], U8, "xo_plane")
+        xt_plane = new([P, T], U8, "xt_plane")
+        wa_plane = new([P, 2 * R], U8, "wa_plane")
+        w2_plane = new([P, R], U8, "w2_plane")
+        vs_plane = new([P, S], U8, "vs_plane")
+        for plane in (xo_plane, xt_plane, wa_plane, w2_plane, vs_plane):
+            nc.vector.memset(plane[:].bitcast(I32), 0)
+        boards = [new([P, C], F32, f"board{t}") for t in range(PACK)]
+        pages = [new([P, E], F32, f"page{h}") for h in range(N // P)]
+        for zeroed in boards + pages:
+            nc.vector.memset(zeroed[:], 0.0)
+
+        lst2 = load_list(offs2, "lst2")
+        xo_w = load_words(xo_words, Z, U32, "xo_w")
+        lst1 = load_list(offs, "lst1")
+        load_plane(nc.scalar, xo_plane[:], xo_scales)
+        load_plane(nc.scalar, xt_plane[:], xt_scales)
+        xt_w = load_words(xt_words, T, U16, "xt_w")
+        w_w = load_words(w_words, R, U32, "w_w")
+        w0_w = load_words(w0_words, R, U32, "w0_w")
+        load_plane(nc.scalar, wa_plane[:, 0:R], w_scales)
+        load_plane(nc.scalar, wa_plane[:, R : 2 * R], w0_scales)
+        lst3 = load_list(offs3, "lst3")
+        w2_w = load_words(w2_words, R, U32, "w2_w")
+        load_plane(nc.sync, w2_plane[:], w2_scales)
+        lst5 = load_list(offs5, "lst5")
+        lst4 = load_list(offs4, "lst4")
+        vs_w = load_words(vs_words, S, U32, "vs_w")
+        lst6 = load_list(offs6, "lst6")
+        load_plane(nc.sync, vs_plane[:], vs_scales)
+        lst7 = load_list(offs7, "lst7")
+
+        def gather(table, lst, count, dtype, name):
+            picked = new([P, count], dtype, name)
+            nc.vector.tensor_copy(picked[:], table[:].indirect(lst[:]))
+            return picked
+
+        xo_gs = gather(xo_plane, lst2, J, U8, "xo_gs")
+        xo_gw = gather(xo_w, lst2, J, U32, "xo_gw")
+        xt_gs = gather(xt_plane, lst1, J, U8, "xt_gs")
+        xt_gw = gather(xt_w, lst1, J, U16, "xt_gw")
+
+        w_d = new([P, PACK, P], U32, "w_d")
+        w0_d = new([P, PACK, P], U32, "w0_d")
+        w2_d = new([P, PACK, P], U32, "w2_d")
+        wa_sd = new([P, PACK, 2, P], U8, "wa_sd")
+        w2_sd = new([P, PACK, P], U8, "w2_sd")
+
+        def deal_words(dealt, words, t0, t1):
+            nc.scalar.copy(
+                dealt[:, t0:t1, :].rearrange("p t m -> p m t"),
+                words[:].rearrange("p (m t) -> p m t", t=PACK)[:, :, t0:t1],
+            )
+
+        def deal_wa_scales(t0, t1):
+            nc.vector.tensor_copy(
+                wa_sd[:, t0:t1, :, :],
+                wa_plane[:].rearrange("p (u m t) -> p t u m", u=2, t=PACK)[:, t0:t1, :, :],
+            )
+
+        deal_words(w_d, w_w, 0, PACK)
+        deal_words(w0_d, w0_w, 0, 1)
+        deal_wa_scales(0, 1)
+
+        a_sb = [new([P, J], F32, f"a{t}") for t in range(PACK)]
+        b_sb = [new([P, J], F32, f"b{t}") for t in range(PACK)]
+
+        def make_a(t):
+            acc = psum.tile([P, J], F32, name=f"a_acc{t}")
+            nc.tensor.matmul_mx(
+                out=acc[:], lhsT=w0_d[:, t, :].bitcast(E4M3), lhsT_scale=wa_sd[:, t, 1, :],
+                rhs=xo_gw[:].bitcast(E5M2), rhs_scale=xo_gs[:], start=True, stop=False,
+            )
+            nc.tensor.matmul_mx(
+                out=acc[:], lhsT=w_d[:, t, :].bitcast(E5M2), lhsT_scale=wa_sd[:, t, 0, :],
+                rhs=xt_gw[:].bitcast(E2M1), rhs_scale=xt_gs[:], start=False, stop=True,
+            )
+            nc.scalar.copy(a_sb[t][:], acc[:])
+            nc.vector.tensor_copy(boards[t][:].indirect(lst3[:]), a_sb[t][:])
+
+        make_a(0)
+        deal_words(w0_d, w0_w, 1, PACK)
+        deal_wa_scales(1, PACK)
+        for t in range(1, PACK):
+            make_a(t)
+
+        deal_words(w2_d, w2_w, 0, PACK)
+        nc.vector.tensor_copy(w2_sd[:], w2_plane[:].rearrange("p (m t) -> p t m", t=PACK))
+        b_acc = [psum.tile([P, 2, J], F32, name=f"b_acc{u}") for u in range(PACK // 2)]
+        for t in range(PACK):
+            nc.tensor.matmul_mx(
+                out=b_acc[t // 2][:, t % 2, :], lhsT=w2_d[:, t, :].bitcast(E4M3), lhsT_scale=w2_sd[:, t, :],
+                rhs=xo_gw[:].bitcast(E5M2), rhs_scale=xo_gs[:], start=True, stop=True,
+            )
+        for t in range(PACK):
+            nc.scalar.copy(b_sb[t][:], b_acc[t // 2][:, t % 2, :])
+
+        from_board = new([P, PACK, O], F32, "from_board")
+        from_b = new([P, PACK, O], F32, "from_b")
+        diff = new([P, PACK, O], F32, "diff")
+        for t in range(PACK):
+            nc.scalar.activation(from_b[:, t, :], b_sb[t][:].indirect(lst5[:]), ACT.Copy, scale=a_sb[t][:, 0:1])
+        for t in range(PACK):
+            nc.scalar.activation(from_board[:, t, :], boards[t][:].indirect(lst4[:]), ACT.Copy, scale=b_sb[t][:, 0:1])
+
+        vs_gs = gather(vs_plane, lst6, N, U8, "vs_gs")
+        vs_gw = gather(vs_w, lst6, N, U32, "vs_gw")
+
+        last = PACK - 1
+        nc.vector.tensor_tensor(diff[:, :last, :], from_board[:, :last, :], from_b[:, :last, :], ALU.subtract)
+        nc.vector.tensor_tensor(diff[:, last, :], from_board[:, last, :], from_b[:, last, :], ALU.subtract)
+        hid = new([P, O, PACK], BF16, "hid")
+        nc.scalar.activation(hid[:], diff[:].rearrange("p t o -> p o t"), ACT.Abs)
+        hid_w = new([P, O], U32, "hid_w")
+        hid_s = new([P, O], U8, "hid_s")
+        nc.vector.quantize_mx(out=hid_w[:].bitcast(E5M2), scales=hid_s[:], in_=hid[:].rearrange("p o t -> p (o t)"))
+
+        for h in range(N // P):
+            cols = slice(h * P, (h + 1) * P)
+            p_acc = psum.tile([P, O], F32, name=f"p_acc{h}")
+            nc.tensor.matmul_mx(
+                out=p_acc[:], lhsT=vs_gw[:, cols].bitcast(E4M3), lhsT_scale=vs_gs[:, cols],
+                rhs=hid_w[:].bitcast(E5M2), rhs_scale=hid_s[:], start=True, stop=True,
+            )
+            p_sb = new([P, O], F32, f"p{h}")
+            if h == 0:
+                nc.vector.tensor_copy(p_sb[:], p_acc[:])
+                nc.vector.tensor_copy(pages[h][:].indirect(lst7[:]), p_sb[:])
+                nc.sync.dma_start(out[cols, :], pages[h][:])
+            else:
+                nc.scalar.copy(p_sb[:], p_acc[:])
+                nc.scalar.activation(pages[h][:].indirect(lst7[:]), p_sb[:], ACT.Copy)
+                nc.scalar.dma_start(out[cols, :], pages[h][:])

@@ -31,8 +31,8 @@ def tile_list_leadgroupboard_noted_store_scattered_kernel(
         keep = ctx.enter_context(tc.tile_pool(name="keep", bufs=1))
         psum = ctx.enter_context(tc.psum_pool(name="psum", bufs=1))
 
-        def new(shape, dtype, name):
-            return keep.tile(shape, dtype, name=name, align_bytes=64)
+        def new(shape, dtype, name, tag=None):
+            return keep.tile(shape, dtype, name=name, tag=tag or name, align_bytes=64)
 
         def load_list(src, name):
             lst = keep.tile(list(src.shape), U16, name=name)
@@ -49,28 +49,30 @@ def tile_list_leadgroupboard_noted_store_scattered_kernel(
             for q in range(QUADS):
                 queue.dma_start(plane[32 * q : 32 * q + 4].bitcast(I32), src[0, 4 * q : 4 * q + 4, :].bitcast(I32))
 
+        def load_rows(rows, src):
+            nc.sync.dma_start(rows, src[0].bitcast(I32).rearrange("(q r) c -> r q c", r=4))
+
         xo_plane = new([P, Z], U8, "xo_plane")
         xt_plane = new([P, T], U8, "xt_plane")
         wa_plane = new([P, 2 * R], U8, "wa_plane")
         w2_plane = new([P, R], U8, "w2_plane")
         vs_plane = new([P, S], U8, "vs_plane")
-        for plane in (xo_plane, xt_plane, wa_plane, w2_plane, vs_plane):
+        for plane in (w2_plane, vs_plane, xo_plane, xt_plane, wa_plane):
             nc.vector.memset(plane[:].bitcast(I32), 0)
-        boards = [new([P, C], F32, f"board{t}") for t in range(PACK)]
-        pages = [new([P, E], F32, f"page{h}") for h in range(N // P)]
-        for zeroed in boards + pages:
-            nc.vector.memset(zeroed[:], 0.0)
 
+        xo_rows = new([4, QUADS, Z // 4], I32, "xo_rows")
+        xt_rows = new([4, QUADS, T // 4], I32, "xt_rows")
+        wa_rows = new([4, QUADS, 2 * R // 4], I32, "wa_rows")
+        load_rows(xo_rows[:], xo_scales)
+        load_rows(xt_rows[:], xt_scales)
+        load_rows(wa_rows[:, :, 0 : R // 4], w_scales)
+        load_rows(wa_rows[:, :, R // 4 : 2 * R // 4], w0_scales)
         lst2 = load_list(offs2, "lst2")
-        xo_w = load_words(xo_words, Z, U32, "xo_w")
         lst1 = load_list(offs, "lst1")
-        load_plane(nc.scalar, xo_plane[:], xo_scales)
-        load_plane(nc.scalar, xt_plane[:], xt_scales)
+        xo_w = load_words(xo_words, Z, U32, "xo_w")
         xt_w = load_words(xt_words, T, U16, "xt_w")
-        w_w = load_words(w_words, R, U32, "w_w")
         w0_w = load_words(w0_words, R, U32, "w0_w")
-        load_plane(nc.scalar, wa_plane[:, 0:R], w_scales)
-        load_plane(nc.scalar, wa_plane[:, R : 2 * R], w0_scales)
+        w_w = load_words(w_words, R, U32, "w_w")
         lst3 = load_list(offs3, "lst3")
         w2_w = load_words(w2_words, R, U32, "w2_w")
         load_plane(nc.sync, w2_plane[:], w2_scales)
@@ -81,8 +83,12 @@ def tile_list_leadgroupboard_noted_store_scattered_kernel(
         load_plane(nc.sync, vs_plane[:], vs_scales)
         lst7 = load_list(offs7, "lst7")
 
-        def gather(table, lst, count, dtype, name):
-            picked = new([P, count], dtype, name)
+        for q in range(QUADS):
+            for plane, rows in ((xo_plane, xo_rows), (xt_plane, xt_rows), (wa_plane, wa_rows)):
+                nc.vector.tensor_copy(plane[32 * q : 32 * q + 4].bitcast(I32), rows[:, q, :])
+
+        def gather(table, lst, count, dtype, name, tag=None):
+            picked = new([P, count], dtype, name, tag)
             nc.vector.tensor_copy(picked[:], table[:].indirect(lst[:]))
             return picked
 
@@ -109,9 +115,13 @@ def tile_list_leadgroupboard_noted_store_scattered_kernel(
                 wa_plane[:].rearrange("p (u m t) -> p t u m", u=2, t=PACK)[:, t0:t1, :, :],
             )
 
+        deal_words(w0_d, w0_w, 0, PACK)
         deal_words(w_d, w_w, 0, PACK)
-        deal_words(w0_d, w0_w, 0, 1)
         deal_wa_scales(0, 1)
+
+        boards = [new([P, C], F32, f"board{t}") for t in range(PACK)]
+        for zeroed in boards:
+            nc.vector.memset(zeroed[:], 0.0)
 
         a_sb = [new([P, J], F32, f"a{t}") for t in range(PACK)]
         b_sb = [new([P, J], F32, f"b{t}") for t in range(PACK)]
@@ -130,13 +140,15 @@ def tile_list_leadgroupboard_noted_store_scattered_kernel(
             nc.vector.tensor_copy(boards[t][:].indirect(lst3[:]), a_sb[t][:])
 
         make_a(0)
-        deal_words(w0_d, w0_w, 1, PACK)
         deal_wa_scales(1, PACK)
         for t in range(1, PACK):
             make_a(t)
 
         deal_words(w2_d, w2_w, 0, PACK)
         nc.vector.tensor_copy(w2_sd[:], w2_plane[:].rearrange("p (m t) -> p t m", t=PACK))
+        pages = [new([P, E], F32, f"page{h}", tag) for h, tag in enumerate(("wa_plane", "w2_plane"))]
+        for zeroed in pages:
+            nc.gpsimd.memset(zeroed[:], 0.0)
         b_acc = [psum.tile([P, 2, J], F32, name=f"b_acc{u}") for u in range(PACK // 2)]
         for t in range(PACK):
             nc.tensor.matmul_mx(
@@ -154,14 +166,13 @@ def tile_list_leadgroupboard_noted_store_scattered_kernel(
         for t in range(PACK):
             nc.scalar.activation(from_board[:, t, :], boards[t][:].indirect(lst4[:]), ACT.Copy, scale=b_sb[t][:, 0:1])
 
-        vs_gs = gather(vs_plane, lst6, N, U8, "vs_gs")
-        vs_gw = gather(vs_w, lst6, N, U32, "vs_gw")
-
         last = PACK - 1
         nc.vector.tensor_tensor(diff[:, :last, :], from_board[:, :last, :], from_b[:, :last, :], ALU.subtract)
         nc.vector.tensor_tensor(diff[:, last, :], from_board[:, last, :], from_b[:, last, :], ALU.subtract)
         hid = new([P, O, PACK], BF16, "hid")
         nc.scalar.activation(hid[:], diff[:].rearrange("p t o -> p o t"), ACT.Abs)
+        vs_gs = gather(vs_plane, lst6, N, U8, "vs_gs", "from_board")
+        vs_gw = gather(vs_w, lst6, N, U32, "vs_gw", "from_b")
         hid_w = new([P, O], U32, "hid_w")
         hid_s = new([P, O], U8, "hid_s")
         nc.vector.quantize_mx(out=hid_w[:].bitcast(E5M2), scales=hid_s[:], in_=hid[:].rearrange("p o t -> p (o t)"))

@@ -49,33 +49,30 @@ def tile_list_leadgroupboard_noted_store_scattered_kernel(
             for q in range(QUADS):
                 queue.dma_start(plane[32 * q : 32 * q + 4].bitcast(I32), src[0, 4 * q : 4 * q + 4, :].bitcast(I32))
 
-        def load_rows(rows, src):
-            nc.sync.dma_start(rows, src[0].bitcast(I32).rearrange("(q r) c -> r q c", r=4))
+        def load_rows(src, columns, name):
+            rows = new([4, QUADS, columns // 4], I32, name)
+            nc.scalar.dma_start(rows[:], src[0].bitcast(I32).rearrange("(q r) c -> r q c", r=4))
+            return rows
 
+        w_planes = new([P, 3 * R], U8, "w_planes")
         xo_plane = new([P, Z], U8, "xo_plane")
         xt_plane = new([P, T], U8, "xt_plane")
-        wa_plane = new([P, 2 * R], U8, "wa_plane")
-        w2_plane = new([P, R], U8, "w2_plane")
         vs_plane = new([P, S], U8, "vs_plane")
-        for plane in (w2_plane, vs_plane, xo_plane, xt_plane, wa_plane):
+        for plane in (w_planes, vs_plane, xo_plane, xt_plane):
             nc.vector.memset(plane[:].bitcast(I32), 0)
 
-        xo_rows = new([4, QUADS, Z // 4], I32, "xo_rows")
-        xt_rows = new([4, QUADS, T // 4], I32, "xt_rows")
-        wa_rows = new([4, QUADS, 2 * R // 4], I32, "wa_rows")
-        load_rows(xo_rows[:], xo_scales)
-        load_rows(xt_rows[:], xt_scales)
-        load_rows(wa_rows[:, :, 0 : R // 4], w_scales)
-        load_rows(wa_rows[:, :, R // 4 : 2 * R // 4], w0_scales)
+        xo_rows = load_rows(xo_scales, Z, "xo_rows")
+        xt_rows = load_rows(xt_scales, T, "xt_rows")
         lst2 = load_list(offs2, "lst2")
         lst1 = load_list(offs, "lst1")
         xo_w = load_words(xo_words, Z, U32, "xo_w")
         xt_w = load_words(xt_words, T, U16, "xt_w")
         w0_w = load_words(w0_words, R, U32, "w0_w")
         w_w = load_words(w_words, R, U32, "w_w")
+        for u, src in enumerate((w0_scales, w_scales, w2_scales)):
+            load_plane(nc.sync, w_planes[:, u * R : (u + 1) * R], src)
         lst3 = load_list(offs3, "lst3")
         w2_w = load_words(w2_words, R, U32, "w2_w")
-        load_plane(nc.sync, w2_plane[:], w2_scales)
         lst5 = load_list(offs5, "lst5")
         lst4 = load_list(offs4, "lst4")
         vs_w = load_words(vs_words, S, U32, "vs_w")
@@ -84,7 +81,7 @@ def tile_list_leadgroupboard_noted_store_scattered_kernel(
         lst7 = load_list(offs7, "lst7")
 
         for q in range(QUADS):
-            for plane, rows in ((xo_plane, xo_rows), (xt_plane, xt_rows), (wa_plane, wa_rows)):
+            for plane, rows in ((xo_plane, xo_rows), (xt_plane, xt_rows)):
                 nc.vector.tensor_copy(plane[32 * q : 32 * q + 4].bitcast(I32), rows[:, q, :])
 
         def gather(table, lst, count, dtype, name, tag=None):
@@ -100,27 +97,27 @@ def tile_list_leadgroupboard_noted_store_scattered_kernel(
         w_d = new([P, PACK, P], U32, "w_d")
         w0_d = new([P, PACK, P], U32, "w0_d")
         w2_d = new([P, PACK, P], U32, "w2_d")
-        wa_sd = new([P, PACK, 2, P], U8, "wa_sd")
-        w2_sd = new([P, PACK, P], U8, "w2_sd")
+        w_sd = new([P, 3, PACK, P], U8, "w_sd")
 
         def deal_words(dealt, words, t0, t1):
             nc.scalar.copy(
-                dealt[:, t0:t1, :].rearrange("p t m -> p m t"),
-                words[:].rearrange("p (m t) -> p m t", t=PACK)[:, :, t0:t1],
+                dealt[:, t0:t1, :].rearrange("p t (g m) -> p g t m", m=4),
+                words[:].rearrange("p (g m t) -> p g t m", m=4, t=PACK)[:, :, t0:t1, :],
             )
 
-        def deal_wa_scales(t0, t1):
+        def deal_scales(u0, u1, t0, t1):
             nc.vector.tensor_copy(
-                wa_sd[:, t0:t1, :, :],
-                wa_plane[:].rearrange("p (u m t) -> p t u m", u=2, t=PACK)[:, t0:t1, :, :],
+                w_sd[:, u0:u1, t0:t1, :],
+                w_planes[:].rearrange("p (u m t) -> p u t m", u=3, t=PACK)[:, u0:u1, t0:t1, :],
             )
 
         deal_words(w0_d, w0_w, 0, PACK)
-        deal_words(w_d, w_w, 0, PACK)
-        deal_wa_scales(0, 1)
+        deal_words(w_d, w_w, 0, 1)
+        deal_scales(0, 2, 0, 1)
 
         boards = [new([P, C], F32, f"board{t}") for t in range(PACK)]
-        for zeroed in boards:
+        pages = [new([P, E], F32, f"page{h}") for h in range(N // P)]
+        for zeroed in boards + pages:
             nc.vector.memset(zeroed[:], 0.0)
 
         a_sb = [new([P, J], F32, f"a{t}") for t in range(PACK)]
@@ -129,30 +126,29 @@ def tile_list_leadgroupboard_noted_store_scattered_kernel(
         def make_a(t):
             acc = psum.tile([P, J], F32, name=f"a_acc{t}")
             nc.tensor.matmul_mx(
-                out=acc[:], lhsT=w0_d[:, t, :].bitcast(E4M3), lhsT_scale=wa_sd[:, t, 1, :],
+                out=acc[:], lhsT=w0_d[:, t, :].bitcast(E4M3), lhsT_scale=w_sd[:, 0, t, :],
                 rhs=xo_gw[:].bitcast(E5M2), rhs_scale=xo_gs[:], start=True, stop=False,
             )
             nc.tensor.matmul_mx(
-                out=acc[:], lhsT=w_d[:, t, :].bitcast(E5M2), lhsT_scale=wa_sd[:, t, 0, :],
+                out=acc[:], lhsT=w_d[:, t, :].bitcast(E5M2), lhsT_scale=w_sd[:, 1, t, :],
                 rhs=xt_gw[:].bitcast(E2M1), rhs_scale=xt_gs[:], start=False, stop=True,
             )
             nc.scalar.copy(a_sb[t][:], acc[:])
-            nc.vector.tensor_copy(boards[t][:].indirect(lst3[:]), a_sb[t][:])
 
         make_a(0)
-        deal_wa_scales(1, PACK)
+        deal_words(w_d, w_w, 1, PACK)
+        deal_scales(0, 2, 1, PACK)
+        deal_scales(2, 3, 0, PACK)
         for t in range(1, PACK):
             make_a(t)
+        for t in range(PACK):
+            nc.vector.tensor_copy(boards[t][:].indirect(lst3[:]), a_sb[t][:])
 
         deal_words(w2_d, w2_w, 0, PACK)
-        nc.vector.tensor_copy(w2_sd[:], w2_plane[:].rearrange("p (m t) -> p t m", t=PACK))
-        pages = [new([P, E], F32, f"page{h}", tag) for h, tag in enumerate(("wa_plane", "w2_plane"))]
-        for zeroed in pages:
-            nc.gpsimd.memset(zeroed[:], 0.0)
         b_acc = [psum.tile([P, 2, J], F32, name=f"b_acc{u}") for u in range(PACK // 2)]
         for t in range(PACK):
             nc.tensor.matmul_mx(
-                out=b_acc[t // 2][:, t % 2, :], lhsT=w2_d[:, t, :].bitcast(E4M3), lhsT_scale=w2_sd[:, t, :],
+                out=b_acc[t // 2][:, t % 2, :], lhsT=w2_d[:, t, :].bitcast(E4M3), lhsT_scale=w_sd[:, 2, t, :],
                 rhs=xo_gw[:].bitcast(E5M2), rhs_scale=xo_gs[:], start=True, stop=True,
             )
         for t in range(PACK):

@@ -49,50 +49,58 @@ def tile_list_leadgroupboard_noted_store_scattered_kernel(
             for q in range(QUADS):
                 queue.dma_start(plane[32 * q : 32 * q + 4].bitcast(I32), src[0, 4 * q : 4 * q + 4, :].bitcast(I32))
 
+        def load_halves(queue, halves, src):
+            by_quadrant = src[0].bitcast(I32).rearrange("(h q r) c -> q r h c", h=2, q=2)
+            for q in range(2):
+                queue.dma_start(halves[32 * q : 32 * q + 4], by_quadrant[q])
+
         def load_rows(src, columns, name):
             rows = new([4, QUADS, columns // 4], I32, name)
-            nc.scalar.dma_start(rows[:], src[0].bitcast(I32).rearrange("(q r) c -> r q c", r=4))
+            nc.sync.dma_start(rows[:], src[0].bitcast(I32).rearrange("(q r) c -> r q c", r=4))
             return rows
 
-        w_planes = new([P, 3 * R], U8, "w_planes")
-        xo_plane = new([P, Z], U8, "xo_plane")
+        w_halves = new([P, 2, 3 * R // 4], I32, "w_halves")
+        nc.vector.memset(w_halves[0:64, 0, :], 0)
+        nc.gpsimd.memset(w_halves[0:64, 1, :], 0)
         xt_plane = new([P, T], U8, "xt_plane")
+        xo_plane = new([P, Z], U8, "xo_plane")
         vs_plane = new([P, S], U8, "vs_plane")
-        for plane in (w_planes, vs_plane, xo_plane, xt_plane):
+        for plane in (xt_plane, xo_plane, vs_plane):
             nc.vector.memset(plane[:].bitcast(I32), 0)
 
-        xo_rows = load_rows(xo_scales, Z, "xo_rows")
         xt_rows = load_rows(xt_scales, T, "xt_rows")
-        lst2 = load_list(offs2, "lst2")
+        xo_rows = load_rows(xo_scales, Z, "xo_rows")
         lst1 = load_list(offs, "lst1")
-        xo_w = load_words(xo_words, Z, U32, "xo_w")
         xt_w = load_words(xt_words, T, U16, "xt_w")
+        lst2 = load_list(offs2, "lst2")
+        xo_w = load_words(xo_words, Z, U32, "xo_w")
         w0_w = load_words(w0_words, R, U32, "w0_w")
         w_w = load_words(w_words, R, U32, "w_w")
         for u, src in enumerate((w0_scales, w_scales, w2_scales)):
-            load_plane(nc.sync, w_planes[:, u * R : (u + 1) * R], src)
+            load_halves(nc.sync, w_halves[:, :, u * R // 4 : (u + 1) * R // 4], src)
+        vs_w = load_words(vs_words, S, U32, "vs_w")
+        lst6 = load_list(offs6, "lst6")
         lst3 = load_list(offs3, "lst3")
         w2_w = load_words(w2_words, R, U32, "w2_w")
         lst5 = load_list(offs5, "lst5")
         lst4 = load_list(offs4, "lst4")
-        vs_w = load_words(vs_words, S, U32, "vs_w")
-        lst6 = load_list(offs6, "lst6")
         load_plane(nc.sync, vs_plane[:], vs_scales)
         lst7 = load_list(offs7, "lst7")
-
-        for q in range(QUADS):
-            for plane, rows in ((xo_plane, xo_rows), (xt_plane, xt_rows)):
-                nc.vector.tensor_copy(plane[32 * q : 32 * q + 4].bitcast(I32), rows[:, q, :])
 
         def gather(table, lst, count, dtype, name, tag=None):
             picked = new([P, count], dtype, name, tag)
             nc.vector.tensor_copy(picked[:], table[:].indirect(lst[:]))
             return picked
 
-        xo_gs = gather(xo_plane, lst2, J, U8, "xo_gs")
-        xo_gw = gather(xo_w, lst2, J, U32, "xo_gw")
-        xt_gs = gather(xt_plane, lst1, J, U8, "xt_gs")
+        for q in range(QUADS):
+            for plane, rows in ((xt_plane, xt_rows), (xo_plane, xo_rows)):
+                nc.vector.tensor_copy(plane[32 * q : 32 * q + 4].bitcast(I32), rows[:, q, :])
         xt_gw = gather(xt_w, lst1, J, U16, "xt_gw")
+        xt_gs = gather(xt_plane, lst1, J, U8, "xt_gs")
+        xo_gw = gather(xo_w, lst2, J, U32, "xo_gw")
+        xo_gs = gather(xo_plane, lst2, J, U8, "xo_gs")
+        nc.vector.tensor_copy(w_halves[64:P, 0, :], w_halves[0:64, 1, :])
+        w_planes = w_halves[:, 0, :].bitcast(U8)
 
         w_d = new([P, PACK, P], U32, "w_d")
         w0_d = new([P, PACK, P], U32, "w0_d")
@@ -108,7 +116,7 @@ def tile_list_leadgroupboard_noted_store_scattered_kernel(
         def deal_scales(u0, u1, t0, t1):
             nc.vector.tensor_copy(
                 w_sd[:, u0:u1, t0:t1, :],
-                w_planes[:].rearrange("p (u m t) -> p u t m", u=3, t=PACK)[:, u0:u1, t0:t1, :],
+                w_planes.rearrange("p (u m t) -> p u t m", u=3, t=PACK)[:, u0:u1, t0:t1, :],
             )
 
         deal_words(w0_d, w0_w, 0, PACK)
@@ -116,8 +124,7 @@ def tile_list_leadgroupboard_noted_store_scattered_kernel(
         deal_scales(0, 2, 0, 1)
 
         boards = [new([P, C], F32, f"board{t}") for t in range(PACK)]
-        pages = [new([P, E], F32, f"page{h}") for h in range(N // P)]
-        for zeroed in boards + pages:
+        for zeroed in boards:
             nc.vector.memset(zeroed[:], 0.0)
 
         a_sb = [new([P, J], F32, f"a{t}") for t in range(PACK)]
@@ -139,12 +146,13 @@ def tile_list_leadgroupboard_noted_store_scattered_kernel(
         deal_words(w_d, w_w, 1, PACK)
         deal_scales(0, 2, 1, PACK)
         deal_scales(2, 3, 0, PACK)
-        for t in range(1, PACK):
-            make_a(t)
-        for t in range(PACK):
-            nc.vector.tensor_copy(boards[t][:].indirect(lst3[:]), a_sb[t][:])
+        vs_gw = gather(vs_w, lst6, N, U32, "vs_gw")
+        make_a(1)
 
         deal_words(w2_d, w2_w, 0, PACK)
+        pages = [new([P, E], F32, f"page{h}", tag) for h, tag in enumerate(("w_halves", "w2_w"))]
+        for zeroed in pages:
+            nc.gpsimd.memset(zeroed[:], 0.0)
         b_acc = [psum.tile([P, 2, J], F32, name=f"b_acc{u}") for u in range(PACK // 2)]
         for t in range(PACK):
             nc.tensor.matmul_mx(
@@ -153,6 +161,11 @@ def tile_list_leadgroupboard_noted_store_scattered_kernel(
             )
         for t in range(PACK):
             nc.scalar.copy(b_sb[t][:], b_acc[t // 2][:, t % 2, :])
+
+        for t in range(2, PACK):
+            make_a(t)
+        for t in range(PACK):
+            nc.vector.tensor_copy(boards[t][:].indirect(lst3[:]), a_sb[t][:])
 
         from_board = new([P, PACK, O], F32, "from_board")
         from_b = new([P, PACK, O], F32, "from_b")
@@ -168,7 +181,6 @@ def tile_list_leadgroupboard_noted_store_scattered_kernel(
         hid = new([P, O, PACK], BF16, "hid")
         nc.scalar.activation(hid[:], diff[:].rearrange("p t o -> p o t"), ACT.Abs)
         vs_gs = gather(vs_plane, lst6, N, U8, "vs_gs", "from_board")
-        vs_gw = gather(vs_w, lst6, N, U32, "vs_gw", "from_b")
         hid_w = new([P, O], U32, "hid_w")
         hid_s = new([P, O], U8, "hid_s")
         nc.vector.quantize_mx(out=hid_w[:].bitcast(E5M2), scales=hid_s[:], in_=hid[:].rearrange("p o t -> p (o t)"))

from contextlib import ExitStack

import concourse.mybir as mybir

K, T, J, R, F, Z, C, O, N, S, E = 512, 1024, 256, 512, 512, 1024, 512, 128, 256, 1024, 1024
FLOPS = 2 * K * R * J + 2 * 2 * F * R * J + 2 * R * N * O

F32 = mybir.dt.float32
BF16 = mybir.dt.bfloat16
I32 = mybir.dt.int32
U32 = mybir.dt.uint32
U16 = mybir.dt.uint16
U8 = mybir.dt.uint8
E4M3 = mybir.dt.float8_e4m3fn_x4
E5M2 = mybir.dt.float8_e5m2_x4
E2M1 = mybir.dt.float4_e2m1fn_x4
ACT = mybir.ActivationFunctionType
ALU = mybir.AluOpType

P = 128
PACK = 4
QUADS = 4


def tile_list_leadgroupboard_noted_store_scattered_kernel(
    tc, xt_words, xt_scales, xo_words, xo_scales, w_words, w_scales, w0_words, w0_scales,
    w2_words, w2_scales, vs_words, vs_scales, offs, offs2, offs3, offs4, offs5, offs6, offs7, out,
):
    nc = tc.nc
    with ExitStack() as ctx:
        keep = ctx.enter_context(tc.tile_pool(name="keep", bufs=1))
        psum = ctx.enter_context(tc.psum_pool(name="psum", bufs=1))

        def new(shape, dtype, name, tag=None):
            return keep.tile(shape, dtype, name=name, tag=tag or name, align_bytes=64)

        def load_list(src, name):
            lst = keep.tile(list(src.shape), U16, name=name)
            nc.sync.dma_start(lst[:], src)
            return lst

        def load_words(src, columns, dtype, name):
            words = new([P, columns], dtype, name)
            rows = src[0] if src.ndim == 3 else src[0].rearrange("p n t -> p (n t)")
            nc.sync.dma_start(words[:].bitcast(I32), rows.bitcast(I32))
            return words

        def load_plane(queue, plane, src):
            for q in range(QUADS):
                queue.dma_start(plane[32 * q : 32 * q + 4].bitcast(I32), src[0, 4 * q : 4 * q + 4, :].bitcast(I32))

        def load_halves(queue, halves, src):
            by_quadrant = src[0].bitcast(I32).rearrange("(h q r) c -> q r h c", h=2, q=2)
            for q in range(2):
                queue.dma_start(halves[32 * q : 32 * q + 4], by_quadrant[q])

        def load_rows(src, columns, name):
            rows = new([4, QUADS, columns // 4], I32, name)
            nc.sync.dma_start(rows[:], src[0].bitcast(I32).rearrange("(q r) c -> r q c", r=4))
            return rows

        w_halves = new([P, 2, 3 * R // 4], I32, "w_halves")
        nc.vector.memset(w_halves[0:64, 0, :], 0)
        nc.gpsimd.memset(w_halves[0:64, 1, :], 0)
        xt_plane = new([P, T], U8, "xt_plane")
        xo_plane = new([P, Z], U8, "xo_plane")
        vs_plane = new([P, S], U8, "vs_plane")
        for plane in (xt_plane, xo_plane, vs_plane):
            nc.vector.memset(plane[:].bitcast(I32), 0)

        xt_rows = load_rows(xt_scales, T, "xt_rows")
        xo_rows = load_rows(xo_scales, Z, "xo_rows")
        lst1 = load_list(offs, "lst1")
        xt_w = load_words(xt_words, T, U16, "xt_w")
        lst2 = load_list(offs2, "lst2")
        xo_w = load_words(xo_words, Z, U32, "xo_w")
        w0_w = load_words(w0_words, R, U32, "w0_w")
        w_w = load_words(w_words, R, U32, "w_w")
        for u, src in enumerate((w0_scales, w_scales, w2_scales)):
            load_halves(nc.sync, w_halves[:, :, u * R // 4 : (u + 1) * R // 4], src)
        vs_w = load_words(vs_words, S, U32, "vs_w")
        lst6 = load_list(offs6, "lst6")
        lst3 = load_list(offs3, "lst3")
        w2_w = load_words(w2_words, R, U32, "w2_w")
        lst5 = load_list(offs5, "lst5")
        lst4 = load_list(offs4, "lst4")
        load_plane(nc.sync, vs_plane[:], vs_scales)
        lst7 = load_list(offs7, "lst7")

        def gather(table, lst, count, dtype, name, tag=None):
            picked = new([P, count], dtype, name, tag)
            nc.vector.tensor_copy(picked[:], table[:].indirect(lst[:]))
            return picked

        for q in range(QUADS):
            for plane, rows in ((xt_plane, xt_rows), (xo_plane, xo_rows)):
                nc.vector.tensor_copy(plane[32 * q : 32 * q + 4].bitcast(I32), rows[:, q, :])
        xt_gw = gather(xt_w, lst1, J, U16, "xt_gw")
        xt_gs = gather(xt_plane, lst1, J, U8, "xt_gs")
        xo_gw = gather(xo_w, lst2, J, U32, "xo_gw")
        xo_gs = gather(xo_plane, lst2, J, U8, "xo_gs")
        nc.vector.tensor_copy(w_halves[64:P, 0, :], w_halves[0:64, 1, :])
        w_planes = w_halves[:, 0, :].bitcast(U8)

        w_d = new([P, PACK, P], U32, "w_d")
        w0_d = new([P, PACK, P], U32, "w0_d")
        w2_d = new([P, PACK, P], U32, "w2_d")
        w_sd = new([P, 3, PACK, P], U8, "w_sd")

        def deal_words(dealt, words, t0, t1):
            nc.scalar.copy(
                dealt[:, t0:t1, :].rearrange("p t (g m) -> p g t m", m=4),
                words[:].rearrange("p (g m t) -> p g t m", m=4, t=PACK)[:, :, t0:t1, :],
            )

        def deal_scales(u0, u1, t0, t1):
            nc.vector.tensor_copy(
                w_sd[:, u0:u1, t0:t1, :],
                w_planes.rearrange("p (u m t) -> p u t m", u=3, t=PACK)[:, u0:u1, t0:t1, :],
            )

        deal_words(w0_d, w0_w, 0, PACK)
        deal_words(w_d, w_w, 0, 1)
        deal_scales(0, 2, 0, 1)

        boards = [new([P, C], F32, f"board{t}") for t in range(PACK)]
        for zeroed in boards:
            nc.vector.memset(zeroed[:], 0.0)

        a_sb = [new([P, J], F32, f"a{t}") for t in range(PACK)]
        b_sb = [new([P, J], F32, f"b{t}") for t in range(PACK)]

        def make_a(t):
            acc = psum.tile([P, J], F32, name=f"a_acc{t}")
            nc.tensor.matmul_mx(
                out=acc[:], lhsT=w0_d[:, t, :].bitcast(E4M3), lhsT_scale=w_sd[:, 0, t, :],
                rhs=xo_gw[:].bitcast(E5M2), rhs_scale=xo_gs[:], start=True, stop=False,
            )
            nc.tensor.matmul_mx(
                out=acc[:], lhsT=w_d[:, t, :].bitcast(E5M2), lhsT_scale=w_sd[:, 1, t, :],
                rhs=xt_gw[:].bitcast(E2M1), rhs_scale=xt_gs[:], start=False, stop=True,
            )
            nc.scalar.copy(a_sb[t][:], acc[:])

        make_a(0)
        deal_words(w_d, w_w, 1, PACK)
        deal_scales(0, 2, 1, PACK)
        deal_scales(2, 3, 0, PACK)
        vs_gw = gather(vs_w, lst6, N, U32, "vs_gw")
        make_a(1)

        deal_words(w2_d, w2_w, 0, PACK)
        pages = [new([P, E], F32, f"page{h}", tag) for h, tag in enumerate(("w_halves", "w2_w"))]
        for zeroed in pages:
            nc.gpsimd.memset(zeroed[:], 0.0)
        b_acc = [psum.tile([P, 2, J], F32, name=f"b_acc{u}") for u in range(PACK // 2)]
        for t in range(PACK):
            nc.tensor.matmul_mx(
                out=b_acc[t // 2][:, t % 2, :], lhsT=w2_d[:, t, :].bitcast(E4M3), lhsT_scale=w_sd[:, 2, t, :],
                rhs=xo_gw[:].bitcast(E5M2), rhs_scale=xo_gs[:], start=True, stop=True,
            )
        for t in range(PACK):
            nc.scalar.copy(b_sb[t][:], b_acc[t // 2][:, t % 2, :])

        for t in range(2, PACK):
            make_a(t)
        for t in range(PACK):
            nc.vector.tensor_copy(boards[t][:].indirect(lst3[:]), a_sb[t][:])

        from_board = new([P, PACK, O], F32, "from_board")
        from_b = new([P, PACK, O], F32, "from_b")
        diff = new([P, PACK, O], F32, "diff")
        for t in range(PACK):
            nc.scalar.activation(from_b[:, t, :], b_sb[t][:].indirect(lst5[:]), ACT.Copy, scale=a_sb[t][:, 0:1])
        for t in range(PACK):
            nc.scalar.activation(from_board[:, t, :], boards[t][:].indirect(lst4[:]), ACT.Copy, scale=b_sb[t][:, 0:1])

        last = PACK - 1
        nc.vector.tensor_tensor(diff[:, :last, :], from_board[:, :last, :], from_b[:, :last, :], ALU.subtract)
        nc.vector.tensor_tensor(diff[:, last, :], from_board[:, last, :], from_b[:, last, :], ALU.subtract)
        hid = new([P, O, PACK], BF16, "hid")
        nc.scalar.activation(hid[:], diff[:].rearrange("p t o -> p o t"), ACT.Abs)
        vs_gs = gather(vs_plane, lst6, N, U8, "vs_gs", "from_board")
        hid_w = new([P, O], U32, "hid_w")
        hid_s = new([P, O], U8, "hid_s")
        nc.vector.quantize_mx(out=hid_w[:].bitcast(E5M2), scales=hid_s[:], in_=hid[:].rearrange("p o t -> p (o t)"))

        for h in range(N // P):
            cols = slice(h * P, (h + 1) * P)
            p_acc = psum.tile([P, O], F32, name=f"p_acc{h}")
            nc.tensor.matmul_mx(
                out=p_acc[:], lhsT=vs_gw[:, cols].bitcast(E4M3), lhsT_scale=vs_gs[:, cols],
                rhs=hid_w[:].bitcast(E5M2), rhs_scale=hid_s[:], start=True, stop=True,
            )
            p_sb = new([P, O], F32, f"p{h}")
            if h == 0:
                nc.vector.tensor_copy(p_sb[:], p_acc[:])
                nc.vector.tensor_copy(pages[h][:].indirect(lst7[:]), p_sb[:])
                nc.sync.dma_start(out[cols, :], pages[h][:])
            else:
                nc.scalar.copy(p_sb[:], p_acc[:])
                nc.scalar.activation(pages[h][:].indirect(lst7[:]), p_sb[:], ACT.Copy)
                nc.scalar.dma_start(out[cols, :], pages[h][:])
